import numpy as np
import ml_dtypes

BF16 = ml_dtypes.bfloat16


def bf(x):
    return np.asarray(x, np.float32).astype(BF16)


def f32(x):
    return np.asarray(x, np.float32)


def f64(x):
    return np.asarray(x).astype(np.float64)


def striped(idx):
    return np.tile(idx.reshape(-1, 16).T, (8, 1))


def rows(idx, k):
    return np.tile(idx, (k, 1))


def look(tab, idx):
    return np.take_along_axis(f64(tab), rows(idx, len(tab)), axis=1)


K, S, V, N, M = 256, 2048, 512, 512, 512


def setup_inputs():
    return {"tab": f32(np.random.standard_normal((K, S))), "w": bf(np.random.standard_normal((K, M)) / np.sqrt(K)), "offs": striped(np.random.randint(0, S, N))}


def reference(tab, w, offs):
    idx = offs[:16].T.reshape(-1)
    t = look(tab, idx)
    x = np.minimum(np.maximum(t, -1.25), 1.0)
    y = f64(w).T @ x
    return y

@@ -1,0 +1,56 @@
+import concourse.mybir as mybir
+
+P = 128
+R, T = 256, 2048
+N = 512
+M = 512
+LOW, HIGH = -1.25, 1.0
+
+R_BLOCKS = R // P
+M_BLOCKS = M // P
+
+FLOPS = 2 * R * M * N
+
+F32, BF16, U16 = mybir.dt.float32, mybir.dt.bfloat16, mybir.dt.uint16
+MAX, MIN = mybir.AluOpType.max, mybir.AluOpType.min
+
+
+def tile_lookup_deq_clip_none_kernel(tc, tab, w, offs, out):
+    nc = tc.nc
+    with (
+        tc.tile_pool(name="held", bufs=1) as held,
+        tc.psum_pool(name="psum", bufs=1) as psum,
+    ):
+        offsets = held.tile([P, N // 16], U16, name="offsets")
+        nc.sync.dma_start(offsets[:], offs)
+
+        tables = [held.tile([P, T], F32, name=f"table{r}") for r in range(R_BLOCKS)]
+        for r in range(R_BLOCKS):
+            nc.sync.dma_start(tables[r][:], tab[r * P : (r + 1) * P, :])
+
+        weights = [held.tile([P, M], BF16, name=f"weights{r}") for r in range(R_BLOCKS)]
+        for r in range(R_BLOCKS):
+            nc.scalar.dma_start(weights[r][:], w[r * P : (r + 1) * P, :])
+
+        sums = [psum.tile([P, N], F32, name=f"sum{m}") for m in range(M_BLOCKS)]
+        for r in range(R_BLOCKS):
+            clamped = held.tile([P, N], F32, name=f"clamped{r}")
+            nc.vector.tensor_scalar(clamped[:], tables[r][:].indirect(offsets[:]), LOW, HIGH, MAX, MIN)
+            x = held.tile([P, N], BF16, name=f"x{r}")
+            nc.scalar.copy(x[:], clamped[:])
+            for m in range(M_BLOCKS):
+                nc.tensor.matmul(
+                    sums[m][:],
+                    weights[r][:, m * P : (m + 1) * P],
+                    x[:],
+                    start=(r == 0),
+                    stop=(r == R_BLOCKS - 1),
+                )
+
+        for m in range(M_BLOCKS):
+            result = held.tile([P, N], F32, name=f"result{m}")
+            if m % 2 == 0:
+                nc.vector.tensor_copy(result[:], sums[m][:])
+            else:
+                nc.scalar.copy(result[:], sums[m][:])
+            nc.sync.dma_start(out[m * P : (m + 1) * P, :], result[:])

@@ -8,6 +8,7 @@ LOW, HIGH = -1.25, 1.0
 
 R_BLOCKS = R // P
 M_BLOCKS = M // P
+WARM_UPS = 16
 
 FLOPS = 2 * R * M * N
 
@@ -31,6 +32,12 @@ def tile_lookup_deq_clip_none_kernel(tc, tab, w, offs, out):
         weights = [held.tile([P, M], BF16, name=f"weights{r}") for r in range(R_BLOCKS)]
         for r in range(R_BLOCKS):
             nc.scalar.dma_start(weights[r][:], w[r * P : (r + 1) * P, :])
+
+        zeros = held.tile([P, N], BF16, name="zeros")
+        nc.vector.memset(zeros[:], 0.0)
+        unread = psum.tile([P, N], F32, name="unread")
+        for step in range(WARM_UPS):
+            nc.tensor.matmul(unread[:], zeros[:, :P], zeros[:], start=True, stop=True)
 
         sums = [psum.tile([P, N], F32, name=f"sum{m}") for m in range(M_BLOCKS)]
         for r in range(R_BLOCKS):

@@ -6,9 +6,12 @@ N = 512
 M = 512
 LOW, HIGH = -1.25, 1.0
 
+H = N // 2
+
 R_BLOCKS = R // P
 M_BLOCKS = M // P
-WARM_UPS = 16
+HALVES = N // H
+WARM_UPS = 32
 
 FLOPS = 2 * R * M * N
 
@@ -26,38 +29,44 @@ def tile_lookup_deq_clip_none_kernel(tc, tab, w, offs, out):
         nc.sync.dma_start(offsets[:], offs)
 
         tables = [held.tile([P, T], F32, name=f"table{r}") for r in range(R_BLOCKS)]
-        for r in range(R_BLOCKS):
-            nc.sync.dma_start(tables[r][:], tab[r * P : (r + 1) * P, :])
-
         weights = [held.tile([P, M], BF16, name=f"weights{r}") for r in range(R_BLOCKS)]
         for r in range(R_BLOCKS):
-            nc.scalar.dma_start(weights[r][:], w[r * P : (r + 1) * P, :])
+            nc.sync.dma_start(tables[r][:], tab[r * P : (r + 1) * P, :])
+            nc.sync.dma_start(weights[r][:], w[r * P : (r + 1) * P, :])
 
-        zeros = held.tile([P, N], BF16, name="zeros")
+        sums = [
+            [psum.tile([P, H], F32, name=f"sum{m}_{h}") for h in range(HALVES)] for m in range(M_BLOCKS)
+        ]
+
+        zeros = held.tile([P, H], BF16, name="zeros")
         nc.vector.memset(zeros[:], 0.0)
-        unread = psum.tile([P, N], F32, name="unread")
         for step in range(WARM_UPS):
-            nc.tensor.matmul(unread[:], zeros[:, :P], zeros[:], start=True, stop=True)
+            nc.tensor.matmul(sums[0][0][:], zeros[:, :P], zeros[:], start=True, stop=True)
 
-        sums = [psum.tile([P, N], F32, name=f"sum{m}") for m in range(M_BLOCKS)]
         for r in range(R_BLOCKS):
-            clamped = held.tile([P, N], F32, name=f"clamped{r}")
-            nc.vector.tensor_scalar(clamped[:], tables[r][:].indirect(offsets[:]), LOW, HIGH, MAX, MIN)
-            x = held.tile([P, N], BF16, name=f"x{r}")
-            nc.scalar.copy(x[:], clamped[:])
-            for m in range(M_BLOCKS):
-                nc.tensor.matmul(
-                    sums[m][:],
-                    weights[r][:, m * P : (m + 1) * P],
-                    x[:],
-                    start=(r == 0),
-                    stop=(r == R_BLOCKS - 1),
-                )
+            for h in range(HALVES):
+                half_list = offsets[:, h * (H // 16) : (h + 1) * (H // 16)]
+                clamped = held.tile([P, H], F32, name=f"clamped{r}_{h}")
+                nc.vector.tensor_scalar(clamped[:], tables[r][:].indirect(half_list), LOW, HIGH, MAX, MIN)
+                x = held.tile([P, H], BF16, name=f"x{r}_{h}")
+                if h == 0:
+                    nc.scalar.copy(x[:], clamped[:])
+                else:
+                    nc.vector.tensor_copy(x[:], clamped[:])
+                for m in range(M_BLOCKS):
+                    nc.tensor.matmul(
+                        sums[m][h][:],
+                        weights[r][:, m * P : (m + 1) * P],
+                        x[:],
+                        start=(r == 0),
+                        stop=(r == R_BLOCKS - 1),
+                    )
 
-        for m in range(M_BLOCKS):
-            result = held.tile([P, N], F32, name=f"result{m}")
-            if m % 2 == 0:
-                nc.vector.tensor_copy(result[:], sums[m][:])
-            else:
-                nc.scalar.copy(result[:], sums[m][:])
-            nc.sync.dma_start(out[m * P : (m + 1) * P, :], result[:])
+        for h in range(HALVES):
+            for m in range(M_BLOCKS):
+                result = held.tile([P, H], F32, name=f"result{m}_{h}")
+                if h == 0:
+                    nc.scalar.copy(result[:], sums[m][h][:])
+                else:
+                    nc.vector.tensor_copy(result[:], sums[m][h][:])
+                nc.sync.dma_start(out[m * P : (m + 1) * P, h * H : (h + 1) * H], result[:])

@@ -11,7 +11,6 @@ H = N // 2
 R_BLOCKS = R // P
 M_BLOCKS = M // P
 HALVES = N // H
-WARM_UPS = 32
 
 FLOPS = 2 * R * M * N
 
@@ -37,11 +36,6 @@ def tile_lookup_deq_clip_none_kernel(tc, tab, w, offs, out):
         sums = [
             [psum.tile([P, H], F32, name=f"sum{m}_{h}") for h in range(HALVES)] for m in range(M_BLOCKS)
         ]
-
-        zeros = held.tile([P, H], BF16, name="zeros")
-        nc.vector.memset(zeros[:], 0.0)
-        for step in range(WARM_UPS):
-            nc.tensor.matmul(sums[0][0][:], zeros[:, :P], zeros[:], start=True, stop=True)
 
         for r in range(R_BLOCKS):
             for h in range(HALVES):

@@ -56,11 +56,8 @@ def tile_lookup_deq_clip_none_kernel(tc, tab, w, offs, out):
                         stop=(r == R_BLOCKS - 1),
                     )
 
-        for h in range(HALVES):
-            for m in range(M_BLOCKS):
-                result = held.tile([P, H], F32, name=f"result{m}_{h}")
-                if h == 0:
-                    nc.scalar.copy(result[:], sums[m][h][:])
-                else:
-                    nc.vector.tensor_copy(result[:], sums[m][h][:])
-                nc.sync.dma_start(out[m * P : (m + 1) * P, h * H : (h + 1) * H], result[:])
+        for m in range(M_BLOCKS):
+            result = held.tile([P, N], F32, name=f"result{m}")
+            nc.scalar.copy(result[:, :H], sums[m][0][:])
+            nc.vector.tensor_copy(result[:, H:], sums[m][1][:])
+            nc.sync.dma_start(out[m * P : (m + 1) * P, :], result[:])

import concourse.mybir as mybir

P = 128
R, T = 256, 2048
N = 512
M = 512
LOW, HIGH = -1.25, 1.0

H = N // 2

R_BLOCKS = R // P
M_BLOCKS = M // P
HALVES = N // H

FLOPS = 2 * R * M * N

F32, BF16, U16 = mybir.dt.float32, mybir.dt.bfloat16, mybir.dt.uint16
MAX, MIN = mybir.AluOpType.max, mybir.AluOpType.min


def tile_lookup_deq_clip_none_kernel(tc, tab, w, offs, out):
    nc = tc.nc
    with (
        tc.tile_pool(name="held", bufs=1) as held,
        tc.psum_pool(name="psum", bufs=1) as psum,
    ):
        offsets = held.tile([P, N // 16], U16, name="offsets")
        nc.sync.dma_start(offsets[:], offs)

        tables = [held.tile([P, T], F32, name=f"table{r}") for r in range(R_BLOCKS)]
        weights = [held.tile([P, M], BF16, name=f"weights{r}") for r in range(R_BLOCKS)]
        for r in range(R_BLOCKS):
            nc.sync.dma_start(tables[r][:], tab[r * P : (r + 1) * P, :])
            nc.sync.dma_start(weights[r][:], w[r * P : (r + 1) * P, :])

        sums = [
            [psum.tile([P, H], F32, name=f"sum{m}_{h}") for h in range(HALVES)] for m in range(M_BLOCKS)
        ]

        for r in range(R_BLOCKS):
            for h in range(HALVES):
                half_list = offsets[:, h * (H // 16) : (h + 1) * (H // 16)]
                clamped = held.tile([P, H], F32, name=f"clamped{r}_{h}")
                nc.vector.tensor_scalar(clamped[:], tables[r][:].indirect(half_list), LOW, HIGH, MAX, MIN)
                x = held.tile([P, H], BF16, name=f"x{r}_{h}")
                if h == 0:
                    nc.scalar.copy(x[:], clamped[:])
                else:
                    nc.vector.tensor_copy(x[:], clamped[:])
                for m in range(M_BLOCKS):
                    nc.tensor.matmul(
                        sums[m][h][:],
                        weights[r][:, m * P : (m + 1) * P],
                        x[:],
                        start=(r == 0),
                        stop=(r == R_BLOCKS - 1),
                    )

        for m in range(M_BLOCKS):
            result = held.tile([P, N], F32, name=f"result{m}")
            nc.scalar.copy(result[:, :H], sums[m][0][:])
            nc.vector.tensor_copy(result[:, H:], sums[m][1][:])
            nc.sync.dma_start(out[m * P : (m + 1) * P, :], result[:])
